import numpy as np
CORES = [3,67,11,75,19,83,27,91,35,99,43,107,51,115,59,123]
N = 16
T = 128
ROUTE = [[[15,1],[1,9],[2,8],[1,8],[10,8],[2,10],[4,8],[13,6],[7,13],[10,5],[4,7],[0,3],[2,10],[0,15],[2,7],[3,2],[3,5],[14,1],[0,4],[1,2],[4,12],[3,9],[10,15],[2,12],[12,13],[15,14],[5,0],[13,12],[8,10],[11,2],[4,12],[6,12],[8,13],[3,4],[9,2],[15,2],[0,14],[1,10],[0,13],[14,12],[0,8],[5,4],[9,2],[3,9],[10,13],[15,5],[5,15],[3,15],[1,2],[7,8],[7,15],[8,5],[7,15],[2,7],[14,9],[8,1],[3,6],[4,15],[13,12],[15,7],[14,1],[11,3],[13,5],[1,10],[10,1],[5,11],[9,10],[7,9],[7,8],[3,10],[14,9],[6,11],[0,4],[8,6],[7,10],[9,15],[3,15],[11,3],[0,8],[3,7],[1,0],[10,4],[1,15],[4,3],[12,14],[9,10],[3,15],[15,13],[14,11],[3,2],[1,6],[4,12],[11,3],[11,13],[9,11],[9,5],[8,3],[14,1],[12,6],[6,10],[8,2],[10,14],[7,14],[5,0],[8,9],[3,15],[0,15],[2,10],[4,14],[15,0],[7,12],[0,5],[8,10],[8,2],[14,10],[6,3],[2,4],[5,6],[6,12],[8,3],[1,13],[7,12],[6,15],[1,10],[1,3],[5,6],[13,12],[0,2]],[[12,2],[3,8],[12,2],[10,3],[2,4],[2,15],[3,8],[13,0],[5,3],[13,15],[9,0],[3,0],[2,9],[1,11],[12,14],[0,3],[12,2],[6,11],[0,2],[10,0],[9,10],[4,0],[8,3],[9,13],[13,5],[15,12],[3,12],[5,6],[13,11],[13,1],[2,7],[7,6],[1,11],[5,7],[4,0],[7,4],[5,1],[5,12],[8,3],[5,11],[15,10],[11,9],[9,12],[10,2],[6,13],[5,8],[7,5],[1,5],[4,5],[9,8],[1,13],[11,14],[2,5],[0,13],[7,8],[3,10],[10,2],[14,15],[6,3],[9,12],[1,2],[10,1],[4,0],[14,6],[9,12],[12,3],[15,10],[6,14],[6,9],[0,13],[1,9],[7,10],[7,3],[1,5],[15,3],[3,6],[10,15],[13,3],[12,10],[5,11],[8,7],[5,9],[15,0],[8,4],[8,10],[7,1],[15,11],[2,0],[1,9],[5,7],[14,1],[7,15],[11,4],[10,14],[13,12],[9,2],[0,10],[14,3],[7,6],[4,15],[6,3],[7,10],[15,6],[3,7],[7,3],[0,13],[15,13],[4,13],[8,0],[14,2],[1,15],[5,2],[0,13],[1,14],[3,7],[6,10],[14,12],[1,8],[4,13],[11,15],[3,7],[1,9],[14,15],[13,10],[10,15],[7,13],[5,9],[4,2]],[[14,3],[11,15],[13,12],[5,3],[0,10],[4,12],[2,14],[2,12],[9,8],[14,13],[9,1],[7,3],[13,15],[9,0],[10,7],[3,13],[7,3],[6,1],[4,7],[0,8],[0,13],[5,15],[9,13],[0,1],[11,8],[2,13],[11,12],[0,2],[6,7],[3,8],[9,12],[14,15],[1,13],[14,1],[5,1],[8,10],[15,10],[0,15],[4,2],[2,10],[5,8],[5,15],[2,0],[10,9],[8,6],[5,15],[15,8],[1,7],[15,9],[9,11],[0,11],[2,1],[3,12],[10,6],[6,9],[1,3],[10,2],[6,7],[9,10],[9,7],[4,15],[7,15],[6,1],[3,4],[14,6],[15,11],[12,15],[6,9],[15,11],[12,11],[10,7],[0,12],[0,11],[12,13],[5,6],[4,13],[4,5],[11,1],[5,14],[4,3],[8,3],[0,5],[15,9],[0,7],[4,3],[7,1],[7,2],[11,7],[11,6],[7,8],[3,12],[1,0],[14,2],[14,0],[5,9],[3,13],[6,8],[15,14],[15,1],[5,13],[1,8],[3,5],[3,8],[15,3],[9,3],[7,4],[14,3],[11,9],[8,3],[12,5],[9,0],[11,12],[4,15],[11,15],[0,14],[11,2],[9,10],[6,1],[9,6],[5,8],[3,7],[9,0],[3,10],[12,5],[3,15],[4,2],[12,11],[8,1]],[[3,5],[7,9],[13,8],[13,14],[12,11],[4,11],[13,12],[9,12],[10,9],[15,14],[9,3],[10,0],[6,8],[15,4],[15,3],[8,10],[2,5],[12,0],[11,9],[7,3],[15,13],[6,0],[4,15],[4,2],[12,15],[1,3],[12,15],[10,8],[6,7],[1,5],[15,11],[13,5],[15,14],[14,5],[3,12],[10,3],[13,10],[10,9],[15,11],[11,0],[5,1],[15,6],[7,15],[12,5],[4,10],[5,15],[0,6],[1,9],[14,1],[10,12],[6,8],[3,11],[10,6],[12,15],[2,7],[15,9],[15,10],[13,9],[0,4],[11,12],[12,8],[14,11],[5,15],[7,9],[6,14],[12,11],[3,13],[6,14],[0,3],[11,8],[10,11],[5,1],[12,9],[12,13],[3,12],[11,2],[3,10],[10,8],[13,11],[4,5],[6,4],[2,6],[0,6],[1,13],[10,14],[15,0],[12,0],[8,11],[5,15],[10,1],[1,4],[6,1],[3,8],[15,4],[0,7],[4,0],[14,10],[3,4],[11,0],[0,5],[8,9],[3,7],[9,8],[5,1],[5,9],[6,5],[15,7],[5,11],[15,9],[4,1],[8,9],[9,5],[2,5],[1,12],[1,10],[6,2],[12,9],[15,1],[13,4],[5,14],[14,7],[14,8],[3,0],[15,4],[3,9],[0,10],[12,13],[14,10]],[[14,13],[14,10],[7,15],[5,15],[6,14],[12,9],[7,15],[7,4],[2,10],[2,10],[10,3],[1,5],[9,3],[1,15],[5,6],[6,5],[2,0],[0,9],[13,2],[10,9],[10,6],[5,9],[15,10],[9,12],[5,4],[12,3],[6,11],[0,4],[12,14],[12,3],[5,1],[4,3],[4,2],[11,6],[9,7],[11,14],[13,2],[0,2],[12,9],[2,0],[1,4],[2,11],[1,13],[0,9],[2,14],[8,14],[4,3],[12,6],[6,1],[11,9],[10,13],[2,7],[1,5],[5,11],[9,15],[2,12],[4,9],[10,6],[14,7],[13,2],[5,8],[4,5],[8,4],[2,0],[5,2],[3,5],[13,3],[14,4],[3,1],[6,1],[13,11],[3,2],[13,1],[5,14],[1,10],[12,5],[10,0],[2,10],[6,14],[1,13],[10,4],[10,5],[4,2],[1,3],[8,10],[15,1],[15,13],[9,8],[7,15],[12,1],[11,1],[15,2],[11,2],[15,0],[13,0],[15,11],[1,5],[1,7],[7,12],[11,5],[5,15],[0,11],[1,14],[6,12],[7,9],[11,8],[12,4],[9,1],[13,9],[15,8],[3,8],[7,14],[2,9],[4,11],[6,14],[12,10],[15,8],[5,11],[0,15],[0,14],[6,4],[1,7],[14,7],[14,13],[13,1],[3,7],[6,11],[11,9]],[[13,10],[11,12],[4,8],[14,4],[14,1],[12,2],[3,10],[8,0],[0,10],[5,1],[15,11],[5,9],[9,12],[8,7],[0,12],[14,9],[8,13],[10,6],[6,9],[5,12],[12,3],[12,14],[13,8],[3,13],[15,9],[4,0],[14,5],[14,4],[7,0],[0,13],[14,2],[0,15],[3,6],[15,3],[8,3],[5,1],[12,11],[13,6],[12,0],[4,9],[4,2],[14,9],[6,8],[2,0],[11,7],[11,14],[12,5],[2,13],[4,9],[10,8],[2,4],[0,10],[15,6],[0,2],[7,4],[1,14],[9,8],[4,1],[5,10],[2,1],[1,10],[5,15],[5,1],[12,9],[10,15],[11,10],[6,15],[14,4],[15,14],[7,4],[10,12],[9,15],[5,12],[1,5],[8,0],[7,10],[14,9],[12,11],[7,9],[10,11],[0,10],[5,1],[8,6],[1,5],[6,10],[5,13],[1,14],[13,1],[1,7],[8,13],[3,8],[11,9],[11,15],[15,14],[8,0],[1,5],[12,11],[2,0],[2,9],[9,3],[9,8],[14,7],[6,13],[8,15],[7,0],[1,14],[6,1],[10,11],[2,15],[14,15],[6,7],[5,14],[6,5],[12,11],[12,3],[4,14],[9,11],[3,5],[4,5],[10,8],[13,10],[11,10],[15,0],[9,2],[4,3],[5,7],[0,1],[13,2]],[[2,5],[3,9],[12,14],[7,5],[14,8],[5,9],[12,14],[13,10],[9,11],[12,5],[0,7],[13,11],[4,3],[6,13],[10,2],[12,6],[13,4],[1,14],[2,6],[10,14],[0,7],[3,1],[0,7],[9,8],[14,15],[0,15],[12,13],[5,10],[2,6],[8,0],[1,12],[14,0],[8,0],[13,10],[1,0],[4,6],[13,11],[1,2],[3,1],[6,14],[14,13],[10,15],[9,4],[12,2],[3,7],[14,13],[2,0],[1,15],[3,13],[11,8],[4,15],[4,11],[2,15],[0,9],[9,13],[13,1],[5,14],[2,13],[15,5],[5,13],[0,12],[9,4],[12,2],[14,7],[8,13],[2,4],[8,2],[3,10],[3,11],[3,2],[9,8],[10,15],[11,8],[8,14],[12,2],[12,8],[15,13],[3,10],[12,6],[7,4],[10,0],[3,13],[2,1],[5,1],[15,7],[0,6],[1,8],[8,13],[13,3],[8,6],[2,13],[15,14],[14,10],[11,15],[12,11],[1,9],[1,11],[2,6],[13,10],[1,4],[12,14],[11,8],[1,7],[13,6],[3,0],[6,11],[2,12],[11,7],[2,8],[4,5],[6,4],[13,3],[5,2],[4,11],[2,13],[4,13],[8,12],[10,7],[7,3],[12,9],[11,1],[14,5],[8,6],[1,11],[0,15],[15,7],[15,5],[11,15]],[[14,15],[1,8],[9,6],[3,7],[1,11],[11,7],[4,13],[11,12],[6,11],[9,0],[7,8],[3,15],[15,4],[6,12],[15,9],[15,11],[9,3],[1,0],[11,4],[3,9],[15,0],[14,1],[0,6],[15,7],[13,10],[0,3],[9,13],[3,6],[3,10],[9,10],[8,12],[0,11],[15,8],[12,14],[4,10],[14,4],[6,8],[2,0],[13,12],[6,5],[7,5],[1,14],[7,15],[8,13],[15,12],[12,11],[3,0],[3,5],[1,15],[5,14],[11,1],[6,0],[3,10],[3,12],[3,6],[4,9],[11,2],[15,3],[9,0],[4,6],[5,1],[12,15],[4,10],[13,12],[1,3],[2,3],[6,11],[7,8],[9,13],[15,9],[12,15],[4,3],[1,12],[15,5],[1,3],[5,2],[5,8],[15,0],[11,6],[1,9],[3,4],[7,3],[10,7],[5,3],[0,7],[14,10],[1,14],[1,8],[4,11],[12,15],[0,1],[11,1],[15,11],[9,12],[10,8],[2,10],[12,9],[11,15],[8,7],[8,4],[0,8],[0,14],[10,7],[8,5],[13,7],[15,12],[9,5],[13,9],[8,3],[11,2],[13,0],[13,6],[2,14],[15,7],[7,10],[0,3],[12,10],[9,7],[7,1],[11,12],[13,0],[0,7],[11,9],[15,11],[5,6],[13,11],[0,4],[6,13]],[[7,11],[6,1],[13,5],[6,10],[5,15],[0,13],[6,12],[9,4],[2,7],[13,12],[9,15],[10,9],[8,7],[9,1],[7,11],[12,0],[12,3],[10,3],[5,0],[13,6],[10,3],[11,6],[13,11],[0,6],[7,6],[1,11],[11,5],[0,13],[5,10],[7,1],[11,0],[11,3],[14,10],[13,8],[0,13],[3,8],[10,13],[10,14],[0,1],[13,14],[11,0],[14,13],[2,0],[14,8],[7,15],[3,8],[0,11],[11,2],[14,9],[4,14],[13,7],[0,13],[11,9],[8,11],[6,1],[9,1],[15,8],[7,10],[5,0],[10,7],[2,15],[2,14],[8,5],[4,15],[13,3],[9,6],[6,9],[0,14],[12,8],[1,14],[2,8],[8,13],[4,13],[8,0],[12,9],[0,2],[12,8],[5,11],[12,7],[13,8],[10,9],[1,10],[14,7],[10,1],[1,9],[15,14],[11,10],[4,2],[5,12],[4,3],[8,6],[9,12],[15,1],[1,8],[7,15],[8,10],[15,12],[15,12],[14,5],[0,2],[5,8],[8,1],[7,10],[3,12],[2,0],[10,4],[7,8],[9,3],[3,15],[3,8],[15,14],[4,8],[1,13],[11,9],[13,6],[4,0],[7,14],[3,15],[7,9],[6,11],[8,0],[12,8],[3,11],[14,3],[4,5],[10,2],[15,12],[12,8]],[[13,0],[14,1],[13,9],[15,8],[0,14],[13,15],[5,2],[1,4],[1,0],[2,4],[0,5],[5,13],[5,15],[2,11],[9,13],[8,3],[14,10],[13,10],[9,10],[9,7],[14,15],[9,10],[8,5],[6,0],[13,0],[5,6],[11,8],[5,1],[15,12],[1,0],[14,7],[4,1],[7,4],[11,8],[2,8],[11,5],[14,4],[6,0],[15,4],[6,11],[3,7],[13,8],[13,7],[4,14],[12,3],[15,5],[1,14],[8,13],[4,9],[5,12],[2,0],[8,0],[14,3],[2,14],[3,0],[11,0],[13,4],[4,7],[2,5],[1,10],[12,9],[7,9],[5,4],[1,8],[0,8],[2,11],[13,3],[10,2],[8,6],[0,9],[1,15],[2,6],[12,11],[6,3],[4,12],[10,0],[8,14],[7,15],[0,13],[12,10],[15,7],[9,3],[0,3],[13,10],[1,12],[14,9],[7,13],[2,8],[2,6],[6,2],[9,7],[12,10],[5,8],[8,0],[2,7],[12,10],[7,2],[12,6],[7,6],[12,2],[10,1],[14,8],[11,13],[12,0],[4,3],[13,9],[6,10],[11,15],[0,3],[4,13],[9,11],[15,13],[6,10],[8,12],[0,11],[10,1],[6,10],[2,10],[9,1],[4,1],[14,7],[13,2],[9,7],[15,3],[0,10],[12,5],[13,5],[3,10]],[[10,14],[13,12],[3,0],[14,4],[2,4],[8,0],[11,2],[8,12],[12,1],[7,12],[14,10],[2,12],[15,10],[5,11],[8,1],[14,3],[14,10],[2,14],[1,13],[14,10],[5,13],[3,6],[1,11],[2,5],[6,1],[0,11],[13,10],[11,1],[8,11],[4,9],[4,11],[3,10],[5,10],[4,9],[8,2],[11,12],[11,6],[10,15],[11,2],[5,6],[8,5],[2,13],[1,10],[8,9],[8,14],[4,6],[6,10],[4,8],[1,13],[8,5],[12,13],[11,5],[7,10],[6,13],[7,4],[9,15],[10,15],[15,8],[0,13],[2,7],[13,5],[1,7],[0,7],[15,13],[12,10],[13,7],[4,6],[11,3],[9,10],[0,5],[6,14],[1,5],[6,4],[5,1],[9,3],[15,3],[11,14],[15,5],[12,15],[5,4],[6,3],[8,5],[6,13],[4,11],[1,0],[15,0],[12,5],[1,15],[15,12],[1,3],[6,2],[9,10],[11,4],[3,9],[1,12],[11,5],[10,1],[12,3],[8,6],[11,9],[8,12],[4,1],[1,15],[12,0],[5,0],[14,10],[6,10],[4,9],[1,10],[0,14],[3,8],[9,14],[11,2],[4,6],[6,15],[1,15],[5,6],[4,2],[11,7],[3,1],[8,9],[7,0],[1,3],[8,3],[10,2],[11,14],[9,1],[11,13]],[[2,8],[11,3],[10,13],[9,1],[14,8],[15,7],[10,11],[3,6],[5,0],[13,3],[13,15],[7,12],[4,2],[2,6],[3,6],[13,6],[7,6],[0,3],[6,15],[9,15],[11,8],[8,2],[7,2],[3,4],[14,9],[8,13],[7,1],[3,2],[15,0],[7,13],[15,4],[2,15],[2,8],[3,13],[2,5],[5,2],[14,9],[11,7],[2,14],[11,14],[5,12],[14,9],[14,2],[15,12],[0,3],[12,13],[4,0],[2,12],[14,8],[8,1],[15,11],[1,6],[1,9],[2,7],[8,9],[2,0],[7,4],[13,11],[10,14],[5,1],[4,15],[9,12],[5,10],[9,5],[7,15],[5,13],[6,3],[0,2],[7,13],[5,1],[12,7],[4,5],[2,8],[8,1],[12,4],[1,8],[9,8],[8,5],[11,1],[10,2],[4,8],[13,7],[5,8],[5,1],[3,10],[15,11],[14,2],[6,14],[15,6],[12,13],[10,15],[13,10],[13,7],[15,12],[3,13],[4,3],[11,10],[11,15],[15,11],[13,7],[6,8],[12,11],[11,13],[2,13],[0,13],[6,10],[6,8],[2,12],[9,7],[6,9],[3,10],[15,9],[1,5],[10,8],[5,4],[7,9],[14,13],[7,1],[4,2],[5,14],[7,15],[6,9],[13,4],[4,5],[5,3],[13,7],[6,8],[12,0]],[[3,1],[14,0],[4,8],[2,1],[5,4],[3,15],[10,2],[8,3],[3,7],[9,7],[14,9],[4,6],[14,7],[12,10],[3,15],[5,9],[4,7],[0,15],[10,15],[5,14],[5,12],[14,9],[8,13],[15,4],[14,10],[6,2],[15,8],[4,5],[5,4],[0,2],[7,14],[0,4],[5,1],[10,9],[8,9],[6,0],[11,13],[4,6],[5,6],[8,11],[6,4],[14,2],[2,5],[13,5],[4,5],[10,0],[12,0],[1,9],[2,11],[9,5],[5,13],[11,13],[7,6],[7,14],[14,12],[3,0],[5,9],[6,2],[2,8],[8,4],[14,11],[13,2],[1,13],[6,2],[10,3],[11,13],[7,15],[13,8],[4,7],[12,10],[10,11],[10,13],[8,4],[12,6],[15,2],[6,4],[15,11],[1,10],[13,2],[15,3],[2,14],[2,6],[8,3],[6,5],[9,2],[7,2],[3,11],[12,5],[7,1],[9,2],[0,4],[12,2],[6,5],[1,8],[15,13],[0,5],[5,8],[10,0],[2,13],[2,11],[7,10],[14,10],[14,8],[15,13],[1,13],[15,10],[9,15],[3,2],[8,4],[8,15],[3,2],[2,3],[4,8],[14,1],[9,15],[0,6],[10,4],[7,1],[14,5],[6,14],[10,4],[3,1],[1,4],[8,13],[1,11],[2,8],[1,0],[7,1]],[[8,11],[0,14],[12,13],[5,8],[9,5],[12,15],[6,15],[9,1],[15,5],[14,15],[2,9],[8,1],[0,2],[1,6],[13,9],[14,0],[13,8],[15,5],[4,2],[7,8],[3,0],[2,9],[1,11],[3,5],[6,10],[5,4],[11,1],[12,8],[4,11],[15,5],[4,11],[11,5],[10,0],[4,3],[5,2],[8,11],[7,14],[9,0],[1,6],[14,15],[15,4],[0,6],[0,1],[0,15],[9,8],[14,9],[4,12],[9,7],[1,4],[7,6],[9,0],[10,4],[0,7],[11,1],[15,9],[15,0],[2,7],[12,4],[6,13],[7,6],[13,1],[13,1],[8,11],[15,7],[12,11],[3,5],[1,14],[5,2],[9,6],[6,7],[15,12],[0,5],[6,4],[13,5],[10,4],[9,5],[7,9],[12,5],[15,12],[15,2],[3,2],[13,15],[7,5],[5,1],[5,8],[3,14],[13,12],[12,14],[14,13],[3,1],[1,2],[13,2],[12,10],[7,0],[4,10],[4,13],[14,15],[7,1],[2,3],[13,12],[12,2],[0,5],[14,11],[9,7],[7,15],[2,15],[10,8],[14,5],[13,11],[1,6],[13,6],[8,15],[9,6],[5,8],[10,13],[3,0],[5,7],[11,9],[13,7],[2,12],[13,10],[2,13],[0,14],[8,9],[14,1],[12,0],[3,2],[3,10]],[[6,15],[7,14],[5,3],[14,6],[15,2],[3,9],[0,1],[2,13],[1,8],[8,0],[5,6],[8,10],[13,8],[10,0],[6,15],[13,12],[2,9],[9,6],[10,6],[6,3],[6,15],[13,0],[5,1],[9,15],[4,3],[2,4],[6,12],[0,15],[4,14],[9,11],[9,12],[14,4],[5,12],[8,3],[0,7],[0,5],[15,5],[14,9],[5,9],[10,1],[7,5],[3,1],[1,12],[14,7],[9,12],[1,6],[7,10],[2,15],[0,12],[4,1],[3,8],[1,2],[10,0],[5,1],[13,9],[7,2],[13,0],[6,10],[9,0],[7,11],[4,6],[2,12],[3,10],[13,4],[4,7],[11,14],[0,7],[13,6],[15,0],[13,11],[0,7],[9,4],[8,9],[1,3],[7,6],[2,9],[3,11],[7,0],[5,6],[2,7],[8,5],[12,8],[0,14],[1,10],[0,8],[3,12],[9,2],[14,7],[12,10],[2,7],[4,10],[6,1],[5,3],[8,7],[4,9],[14,0],[6,0],[0,6],[6,2],[12,9],[10,12],[9,2],[4,12],[15,10],[2,0],[8,12],[12,5],[14,7],[9,3],[5,3],[8,2],[12,11],[5,9],[13,15],[7,14],[15,6],[8,15],[11,2],[1,14],[7,0],[11,4],[15,1],[1,13],[0,15],[5,12],[15,2],[14,11],[8,9]],[[2,14],[6,7],[4,0],[0,1],[15,3],[3,4],[4,10],[12,4],[14,7],[3,11],[15,9],[10,6],[12,13],[14,9],[13,1],[0,9],[6,13],[10,15],[7,8],[2,15],[4,10],[4,10],[10,14],[13,2],[3,10],[13,2],[10,5],[9,1],[14,2],[9,2],[2,11],[5,13],[13,3],[5,8],[8,15],[15,2],[1,15],[6,3],[7,4],[5,10],[2,7],[7,12],[5,3],[4,3],[0,5],[6,9],[5,10],[8,6],[5,7],[9,8],[0,1],[3,8],[13,8],[4,13],[1,9],[1,9],[11,6],[15,14],[7,6],[9,15],[12,5],[2,7],[0,10],[9,7],[7,0],[1,8],[10,6],[1,2],[11,12],[10,13],[3,0],[15,12],[4,12],[13,12],[15,11],[13,4],[9,12],[12,10],[12,10],[8,11],[1,4],[14,4],[3,2],[5,12],[4,15],[10,14],[8,6],[7,10],[11,15],[15,7],[13,11],[13,15],[11,10],[15,4],[10,7],[0,6],[11,5],[4,13],[14,11],[9,15],[5,3],[0,13],[14,7],[8,6],[14,9],[0,8],[1,14],[12,5],[15,9],[10,0],[9,8],[9,6],[7,5],[0,14],[10,1],[7,4],[0,11],[13,3],[12,10],[13,15],[12,9],[1,15],[5,7],[7,14],[2,5],[9,6],[0,10],[8,10]]]
YW = 290
def setup_inputs(rng):
    return {"x": rng.standard_normal((N, 128, T), dtype=np.float32)}
def reference(x):
    y = np.full((N, 128, YW), np.nan, x.dtype)
    fill = [0] * N
    for r in range(N):
        for t in range(T):
            for e in ROUTE[r][t]:
                y[e][:, fill[e]] = x[r][:, t]
                fill[e] += 1
    return {"y": y}

@@ -1,0 +1,179 @@
+from concourse.bass import DstId, RemoteDMATransfer
+
+SCRATCH = {
+    "xs": ("sbuf", [128, 128], "float32"),
+    "pack": ("sbuf", [128, 128], "float32"),
+    "land": ("sbuf", [128, 290], "float32"),
+}
+SEMAPHORES = ["have_x", "pk0", "pk1", "sent", "arrived", "stored"]
+
+_CACHE = {}
+
+
+def runs(ts):
+    out = []
+    for t in ts:
+        if out and out[-1][0] + out[-1][1] == t:
+            out[-1][1] += 1
+        else:
+            out.append([t, 1])
+    return out
+
+
+def engines(mask):
+    return bin(mask).count("1")
+
+
+def make_plan(route, cores, topo):
+    n = len(cores)
+    toks = [[[t for t in range(len(route[r])) if e in route[r][t]] for e in range(n)] for r in range(n)]
+    cnt = [[len(toks[r][e]) for e in range(n)] for r in range(n)]
+    off = [[sum(cnt[q][e] for q in range(r)) for r in range(n)] for e in range(n)]
+    total = [sum(cnt[q][e] for q in range(n)) for e in range(n)]
+    chip = [topo.chip(c) for c in cores]
+    home = {chip[r]: r for r in range(n)}
+
+    def links(r, e):
+        s, c = chip[r], chip[e]
+        if s == c:
+            return []
+        if topo.same_plane(s, c):
+            return [64 + 2 * s, 128 + 2 * c]
+        if topo.mates(s, c):
+            return [2 * s]
+        return [2 * s, 64 + 2 * (s ^ 1), 128 + 2 * c]
+
+    lk = [[links(r, e) for e in range(n)] for r in range(n)]
+    cross = [[(chip[r] ^ chip[e]) & 1 for e in range(n)] for r in range(n)]
+
+    die = [[0] * n for _ in range(n)]
+    for r in range(n):
+        for kind in (0, 1):
+            for i, e in enumerate([e for e in range(n) if cross[r][e] == kind]):
+                die[r][e] = (i + r) & 1
+    ld = [0] * 192
+    for r in range(n):
+        for e in range(n):
+            for l in lk[r][e]:
+                ld[l + die[r][e]] += cnt[r][e]
+
+    def flip(moves):
+        for r, e in moves:
+            for l in lk[r][e]:
+                ld[l + die[r][e]] -= cnt[r][e]
+                ld[l + 1 - die[r][e]] += cnt[r][e]
+            die[r][e] ^= 1
+
+    def score():
+        return (max(ld[64:]), max(ld[:64]), sum(v * v for v in ld))
+
+    best = [score()]
+
+    def attempt(moves):
+        flip(moves)
+        s = score()
+        if s < best[0]:
+            best[0] = s
+            return True
+        flip(moves)
+        return False
+
+    again = True
+    while again:
+        again = False
+        for r in range(n):
+            for a in range(n):
+                for b in range(n):
+                    if cross[r][a] == cross[r][b] and die[r][a] == 1 and die[r][b] == 0:
+                        again = attempt([(r, a), (r, b)]) or again
+        for r in range(n):
+            for q in range(r + 1, n):
+                for a in range(n):
+                    for b in range(a + 1, n):
+                        if (cross[r][a] == cross[r][b] and cross[q][a] == cross[q][b] and die[r][a] != die[r][b]
+                                and die[q][a] != die[q][b] and die[r][a] != die[q][a]):
+                            again = attempt([(r, a), (r, b), (q, a), (q, b)]) or again
+
+    work = {}
+    for r in range(n):
+        base = chip[r] * topo.CORES_PER_CHIP
+        far = (chip[r] ^ 1) * topo.CORES_PER_CHIP
+        for d in (0, 1):
+            mine = [k for k in range(base, base + topo.CORES_PER_CHIP) if topo.die(k) == d]
+            for kind in (0, 1):
+                who = [k for k in mine if topo.may_write(k, far) == (kind == 1)]
+                es = [e for e in range(n) if cross[r][e] == kind and die[r][e] == d]
+                w = [len(runs(toks[r][e])) for e in es]
+                i = min((1, 2, 3), key=lambda j: max(w[0] + w[j], sum(w) - w[0] - w[j]))
+                pairs = [[es[0], es[i]], [es[j] for j in (1, 2, 3) if j != i]]
+                pairs.sort(key=lambda p: sum(len(runs(toks[r][e])) for e in p))
+                who.sort(key=lambda k: k != cores[r])
+                for k, p in zip(who, pairs):
+                    work[k] = p
+    due = [0] * n
+    for k in work:
+        for e in work[k]:
+            if k != cores[e] and cnt[home[topo.chip(k)]][e]:
+                due[e] += engines(topo.mask(k, cores[e]))
+    return {"toks": toks, "off": off, "total": total, "home": home, "work": work, "due": due}
+
+
+def rank_program(g, core, T, topo):
+    if "plan" not in _CACHE:
+        _CACHE["plan"] = make_plan(T.tables["ROUTE"], T.cores, topo)
+    P = _CACHE["plan"]
+    if topo.chip(core) not in P["home"]:
+        return
+    src = P["home"][topo.chip(core)]
+    me = T.rank_of(core)
+    sem = T.sem
+    left = 0
+
+    if me is not None:
+        g.sync.dma_start(T.xs[:], T.x[:]).then_inc(sem.have_x, 16)
+        g.wait_ge(sem.have_x, 16)
+        base = topo.chip(core) * topo.CORES_PER_CHIP
+        peers = [k for k in range(base, base + topo.CORES_PER_CHIP) if k != core]
+        g.remote_dma_fused([RemoteDMATransfer(
+            dst_ids=[DstId(rid=topo.addr(k)[0], pnc=topo.addr(k)[1]) for k in peers],
+            dma_engine_mask=0xFFFF, remote_sem=sem.have_x,
+            srcs=[T.xs[:]], dsts=[T.xs[:] for _k in peers])], local_sem=sem.sent)
+        left += 16
+
+    queues = [(g.sync, sem.pk0), (g.scalar, sem.pk1)]
+    col = 0
+    jobs = []
+    for (q, pk), e in zip(queues, P["work"][core]):
+        ts = P["toks"][src][e]
+        local = T.cores[e] == core
+        buf, at = (T.land, P["off"][e][src]) if local else (T.pack, col)
+        q.wait_ge(sem.have_x, 16)
+        p = at
+        rs = runs(ts)
+        for t, w in rs:
+            q.dma_start(buf[:, p:p + w], T.xs[:, t:t + w]).then_inc(pk, 16)
+            p += w
+        jobs.append((e, pk, 16 * len(rs), at, len(ts), local))
+        if not local:
+            col += len(ts)
+
+    for e, pk, n_pk, at, width, local in jobs:
+        if width == 0:
+            continue
+        g.wait_ge(pk, n_pk)
+        if local:
+            g.sync.wait_ge(pk, n_pk)
+            continue
+        dst = T.cores[e]
+        rid, pid, _ring = topo.addr(dst)
+        m = topo.mask(core, dst)
+        o = P["off"][e][src]
+        g.remote_dma(T.land[:, o:o + width], T.pack[:, at:at + width], sem.arrived, sem.sent, pid, rid, m)
+        left += engines(m)
+
+    if me is not None:
+        g.sync.wait_ge(sem.arrived, P["due"][me])
+        g.sync.dma_start(T.y[:, 0:P["total"][me]], T.land[:, 0:P["total"][me]]).then_inc(sem.stored, 16)
+        g.sync.wait_ge(sem.stored, 16)
+    if left:
+        g.wait_ge(sem.sent, left)

@@ -2,7 +2,7 @@ from concourse.bass import DstId, RemoteDMATransfer
 
 SCRATCH = {
     "xs": ("sbuf", [128, 128], "float32"),
-    "pack": ("sbuf", [128, 128], "float32"),
+    "pack": ("sbuf", [128, 256], "float32"),
     "land": ("sbuf", [128, 290], "float32"),
 }
 SEMAPHORES = ["have_x", "pk0", "pk1", "sent", "arrived", "stored"]
@@ -32,6 +32,8 @@ def make_plan(route, cores, topo):
     total = [sum(cnt[q][e] for q in range(n)) for e in range(n)]
     chip = [topo.chip(c) for c in cores]
     home = {chip[r]: r for r in range(n)}
+    cost = [[len(runs(toks[r][e])) + 1 for e in range(n)] for r in range(n)]
+    extra = topo.CORES_PER_CHIP + 1
 
     def links(r, e):
         s, c = chip[r], chip[e]
@@ -57,15 +59,36 @@ def make_plan(route, cores, topo):
             for l in lk[r][e]:
                 ld[l + die[r][e]] += cnt[r][e]
 
+    def pairing(r, d, kind):
+        es = [e for e in range(n) if cross[r][e] == kind and die[r][e] == d]
+        more = extra if kind == 1 and d == topo.die(cores[r]) else 0
+        best = None
+        for j in (1, 2, 3):
+            a = [es[0], es[j]]
+            b = [es[i] for i in (1, 2, 3) if i != j]
+            if sum(cost[r][e] for e in a) > sum(cost[r][e] for e in b):
+                a, b = b, a
+            v = max(sum(cost[r][e] for e in a) + more, sum(cost[r][e] for e in b))
+            if best is None or v < best[0]:
+                best = (v, a, b)
+        return best
+
+    def busiest(r):
+        return max(pairing(r, d, kind)[0] for d in (0, 1) for kind in (0, 1))
+
+    busy = [busiest(r) for r in range(n)]
+
     def flip(moves):
         for r, e in moves:
             for l in lk[r][e]:
                 ld[l + die[r][e]] -= cnt[r][e]
                 ld[l + 1 - die[r][e]] += cnt[r][e]
             die[r][e] ^= 1
+        for r in sorted(set(r for r, _e in moves)):
+            busy[r] = busiest(r)
 
     def score():
-        return (max(ld[64:]), max(ld[:64]), sum(v * v for v in ld))
+        return (max(ld[64:]), max(ld[:64]), max(busy), sum(v * v for v in ld) + sum(v * v for v in busy))
 
     best = [score()]
 
@@ -102,14 +125,10 @@ def make_plan(route, cores, topo):
             mine = [k for k in range(base, base + topo.CORES_PER_CHIP) if topo.die(k) == d]
             for kind in (0, 1):
                 who = [k for k in mine if topo.may_write(k, far) == (kind == 1)]
-                es = [e for e in range(n) if cross[r][e] == kind and die[r][e] == d]
-                w = [len(runs(toks[r][e])) for e in es]
-                i = min((1, 2, 3), key=lambda j: max(w[0] + w[j], sum(w) - w[0] - w[j]))
-                pairs = [[es[0], es[i]], [es[j] for j in (1, 2, 3) if j != i]]
-                pairs.sort(key=lambda p: sum(len(runs(toks[r][e])) for e in p))
                 who.sort(key=lambda k: k != cores[r])
-                for k, p in zip(who, pairs):
-                    work[k] = p
+                _v, light, heavy = pairing(r, d, kind)
+                work[who[0]] = light
+                work[who[1]] = heavy
     due = [0] * n
     for k in work:
         for e in work[k]:

from concourse.bass import DstId, RemoteDMATransfer

SCRATCH = {
    "xs": ("sbuf", [128, 128], "float32"),
    "pack": ("sbuf", [128, 256], "float32"),
    "land": ("sbuf", [128, 290], "float32"),
}
SEMAPHORES = ["have_x", "pk0", "pk1", "sent", "arrived", "stored"]

_CACHE = {}


def runs(ts):
    out = []
    for t in ts:
        if out and out[-1][0] + out[-1][1] == t:
            out[-1][1] += 1
        else:
            out.append([t, 1])
    return out


def engines(mask):
    return bin(mask).count("1")


def make_plan(route, cores, topo):
    n = len(cores)
    toks = [[[t for t in range(len(route[r])) if e in route[r][t]] for e in range(n)] for r in range(n)]
    cnt = [[len(toks[r][e]) for e in range(n)] for r in range(n)]
    off = [[sum(cnt[q][e] for q in range(r)) for r in range(n)] for e in range(n)]
    total = [sum(cnt[q][e] for q in range(n)) for e in range(n)]
    chip = [topo.chip(c) for c in cores]
    home = {chip[r]: r for r in range(n)}
    cost = [[len(runs(toks[r][e])) + 1 for e in range(n)] for r in range(n)]
    extra = topo.CORES_PER_CHIP + 1

    def links(r, e):
        s, c = chip[r], chip[e]
        if s == c:
            return []
        if topo.same_plane(s, c):
            return [64 + 2 * s, 128 + 2 * c]
        if topo.mates(s, c):
            return [2 * s]
        return [2 * s, 64 + 2 * (s ^ 1), 128 + 2 * c]

    lk = [[links(r, e) for e in range(n)] for r in range(n)]
    cross = [[(chip[r] ^ chip[e]) & 1 for e in range(n)] for r in range(n)]

    die = [[0] * n for _ in range(n)]
    for r in range(n):
        for kind in (0, 1):
            for i, e in enumerate([e for e in range(n) if cross[r][e] == kind]):
                die[r][e] = (i + r) & 1
    ld = [0] * 192
    for r in range(n):
        for e in range(n):
            for l in lk[r][e]:
                ld[l + die[r][e]] += cnt[r][e]

    def pairing(r, d, kind):
        es = [e for e in range(n) if cross[r][e] == kind and die[r][e] == d]
        more = extra if kind == 1 and d == topo.die(cores[r]) else 0
        best = None
        for j in (1, 2, 3):
            a = [es[0], es[j]]
            b = [es[i] for i in (1, 2, 3) if i != j]
            if sum(cost[r][e] for e in a) > sum(cost[r][e] for e in b):
                a, b = b, a
            v = max(sum(cost[r][e] for e in a) + more, sum(cost[r][e] for e in b))
            if best is None or v < best[0]:
                best = (v, a, b)
        return best

    def busiest(r):
        return max(pairing(r, d, kind)[0] for d in (0, 1) for kind in (0, 1))

    busy = [busiest(r) for r in range(n)]

    def flip(moves):
        for r, e in moves:
            for l in lk[r][e]:
                ld[l + die[r][e]] -= cnt[r][e]
                ld[l + 1 - die[r][e]] += cnt[r][e]
            die[r][e] ^= 1
        for r in sorted(set(r for r, _e in moves)):
            busy[r] = busiest(r)

    def score():
        return (max(ld[64:]), max(ld[:64]), max(busy), sum(v * v for v in ld) + sum(v * v for v in busy))

    best = [score()]

    def attempt(moves):
        flip(moves)
        s = score()
        if s < best[0]:
            best[0] = s
            return True
        flip(moves)
        return False

    again = True
    while again:
        again = False
        for r in range(n):
            for a in range(n):
                for b in range(n):
                    if cross[r][a] == cross[r][b] and die[r][a] == 1 and die[r][b] == 0:
                        again = attempt([(r, a), (r, b)]) or again
        for r in range(n):
            for q in range(r + 1, n):
                for a in range(n):
                    for b in range(a + 1, n):
                        if (cross[r][a] == cross[r][b] and cross[q][a] == cross[q][b] and die[r][a] != die[r][b]
                                and die[q][a] != die[q][b] and die[r][a] != die[q][a]):
                            again = attempt([(r, a), (r, b), (q, a), (q, b)]) or again

    work = {}
    for r in range(n):
        base = chip[r] * topo.CORES_PER_CHIP
        far = (chip[r] ^ 1) * topo.CORES_PER_CHIP
        for d in (0, 1):
            mine = [k for k in range(base, base + topo.CORES_PER_CHIP) if topo.die(k) == d]
            for kind in (0, 1):
                who = [k for k in mine if topo.may_write(k, far) == (kind == 1)]
                who.sort(key=lambda k: k != cores[r])
                _v, light, heavy = pairing(r, d, kind)
                work[who[0]] = light
                work[who[1]] = heavy
    due = [0] * n
    for k in work:
        for e in work[k]:
            if k != cores[e] and cnt[home[topo.chip(k)]][e]:
                due[e] += engines(topo.mask(k, cores[e]))
    return {"toks": toks, "off": off, "total": total, "home": home, "work": work, "due": due}


def rank_program(g, core, T, topo):
    if "plan" not in _CACHE:
        _CACHE["plan"] = make_plan(T.tables["ROUTE"], T.cores, topo)
    P = _CACHE["plan"]
    if topo.chip(core) not in P["home"]:
        return
    src = P["home"][topo.chip(core)]
    me = T.rank_of(core)
    sem = T.sem
    left = 0

    if me is not None:
        g.sync.dma_start(T.xs[:], T.x[:]).then_inc(sem.have_x, 16)
        g.wait_ge(sem.have_x, 16)
        base = topo.chip(core) * topo.CORES_PER_CHIP
        peers = [k for k in range(base, base + topo.CORES_PER_CHIP) if k != core]
        g.remote_dma_fused([RemoteDMATransfer(
            dst_ids=[DstId(rid=topo.addr(k)[0], pnc=topo.addr(k)[1]) for k in peers],
            dma_engine_mask=0xFFFF, remote_sem=sem.have_x,
            srcs=[T.xs[:]], dsts=[T.xs[:] for _k in peers])], local_sem=sem.sent)
        left += 16

    queues = [(g.sync, sem.pk0), (g.scalar, sem.pk1)]
    col = 0
    jobs = []
    for (q, pk), e in zip(queues, P["work"][core]):
        ts = P["toks"][src][e]
        local = T.cores[e] == core
        buf, at = (T.land, P["off"][e][src]) if local else (T.pack, col)
        q.wait_ge(sem.have_x, 16)
        p = at
        rs = runs(ts)
        for t, w in rs:
            q.dma_start(buf[:, p:p + w], T.xs[:, t:t + w]).then_inc(pk, 16)
            p += w
        jobs.append((e, pk, 16 * len(rs), at, len(ts), local))
        if not local:
            col += len(ts)

    for e, pk, n_pk, at, width, local in jobs:
        if width == 0:
            continue
        g.wait_ge(pk, n_pk)
        if local:
            g.sync.wait_ge(pk, n_pk)
            continue
        dst = T.cores[e]
        rid, pid, _ring = topo.addr(dst)
        m = topo.mask(core, dst)
        o = P["off"][e][src]
        g.remote_dma(T.land[:, o:o + width], T.pack[:, at:at + width], sem.arrived, sem.sent, pid, rid, m)
        left += engines(m)

    if me is not None:
        g.sync.wait_ge(sem.arrived, P["due"][me])
        g.sync.dma_start(T.y[:, 0:P["total"][me]], T.land[:, 0:P["total"][me]]).then_inc(sem.stored, 16)
        g.sync.wait_ge(sem.stored, 16)
    if left:
        g.wait_ge(sem.sent, left)
